import numpy as np
import ml_dtypes


def mxq(x, axis, fmt="e4m3"):
    dtype, down = {"e4m3": (ml_dtypes.float8_e4m3fn, 7), "e5m2": (ml_dtypes.float8_e5m2, 14)}[fmt]
    v = np.moveaxis(np.asarray(x, np.float32).astype(ml_dtypes.bfloat16).astype(np.float64), axis, -1)
    blocks = v.reshape(v.shape[:-1] + (-1, 32))
    amax = np.abs(blocks).max(-1, keepdims=True)
    byte = np.maximum(np.where(amax > 0, np.frexp(amax)[1] - 1 + 127, 0) - down, 1)
    scale = np.exp2(byte - 127.0)
    codes = (blocks / scale).astype(np.float32).astype(dtype).astype(np.float64)
    return np.moveaxis((codes * scale).reshape(v.shape), -1, axis)


WIDE = False


def mx_kscale(k):
    if not WIDE:
        return np.ones(k)
    levels = np.array([10, -10, 5, -5, 0])
    if k % 512:
        return np.exp2(np.random.permutation(np.resize(levels, k // 32))).repeat(32)
    a = np.empty((k // 512, 16))
    for p in range(k // 512):
        a[p, :8] = np.random.permutation(np.resize(levels, 8))
        for g in range(8):
            far = levels[np.abs(levels - a[p, g]) >= 10]
            a[p, g + 8] = far[np.random.randint(len(far))]
    return np.exp2(a.ravel()).repeat(32)


def f64(x):
    return np.asarray(x).astype(np.float64)


def striped(idx):
    return np.tile(idx.reshape(-1, 16).T, (8, 1)).astype(np.uint16)


def unstriped(offs):
    return offs[:16].T.reshape(-1).astype(np.int64)


def striped8(idx):
    return np.concatenate([x.reshape(-1, 16).T for x in idx]).astype(np.uint16)


def runs(offs, k):
    lists = np.stack([offs[16 * r : 16 * r + 16].T.reshape(-1) for r in range(8)]).astype(np.int64)
    return lists[np.arange(k) % 512 // 64]


def pack_weight(w):
    k, n = w.shape
    w = f64(np.asarray(w, np.float32).astype(ml_dtypes.bfloat16)).reshape(k // 32, 32, n)
    amax = np.abs(w).max(1)
    byte = np.clip(np.where(amax > 0, np.frexp(amax)[1] - 1 + 127 - 7, 1), 1, 254)
    scaled = (w * np.exp2(127.0 - byte)[:, None, :]).reshape(k, n).astype(np.float32)
    words = np.ascontiguousarray(scaled.reshape(k // 512, 128, 4, n).transpose(0, 1, 3, 2)).astype(ml_dtypes.float8_e4m3fn).view(np.uint8)
    return words, np.ascontiguousarray(byte.astype(np.uint8).reshape(k // 512, 16, n))


def unpack_weight(words, scales):
    g, p, n, _ = words.shape
    vals = np.ascontiguousarray(words).view(ml_dtypes.float8_e4m3fn).astype(np.float64) * np.repeat(np.exp2(scales.astype(np.float64) - 127.0), 8, axis=1)[..., None]
    return vals.transpose(0, 1, 3, 2).reshape(g * 512, n)

def planes(y):
    n, m = y.shape
    v = y.astype(np.float32).astype(ml_dtypes.bfloat16).astype(np.float64).reshape(n // 32, 32, m)
    top = np.abs(v).max(1)
    byte = np.clip(np.where(top > 0, np.frexp(top)[1] - 1 + 127 - 7, 1), 1, 254)
    codes = (v * np.exp2(127.0 - byte)[:, None, :]).reshape(n, m).astype(np.float32).astype(ml_dtypes.float8_e4m3fn).view(np.uint8)
    words = codes.reshape(n // 512, 128, 4, m).transpose(0, 1, 3, 2)
    return np.ascontiguousarray(words), np.ascontiguousarray(byte.astype(np.uint8).reshape(n // 512, 16, m))


K, T, S, G, H, W = 512, 1024, 256, 2048, 512, 128


def setup_inputs():
    n = np.random.standard_normal
    s = mx_kscale(K)[:, None]
    packed_xT = pack_weight(n((K, T)) * s)
    packed_dT = pack_weight(n((K, G)) / s)
    perm = np.random.permutation(S)
    perm2 = np.random.permutation(S)
    perm3 = np.random.permutation(S)
    perm4 = np.random.permutation(S)
    return {
        "x_words": packed_xT[0],
        "x_scales": packed_xT[1],
        "d_words": packed_dT[0],
        "d_scales": packed_dT[1],
        "gs": (np.random.uniform(0.5, 1.5, (K, 1)) * s).astype(np.float32),
        "offs": striped(np.random.permutation(T)[:S]),
        "k1": striped8(np.random.randint(0, G, (8, H))),
        "two": striped(np.random.permutation(T)[:S]),
        "k2": striped8(np.random.randint(0, G, (8, H))),
        "n1": striped(perm[:W]),
        "n2": striped(perm[W:]),
        "n3": striped(perm2[:W]),
        "n4": striped(perm2[W:]),
        "n5": striped(np.random.permutation(S)),
        "k3": striped8(np.random.randint(0, G, (8, H))),
        "k4": striped8(np.random.randint(0, G, (8, H))),
        "hz": striped8(np.random.randint(0, T, (8, S))),
        "n6": striped(perm3[:W]),
        "n7": striped(perm3[W:]),
        "n8": striped(perm4[:W]),
        "n9": striped(perm4[W:]),
        "n10": striped(np.random.permutation(S)),
    }


def reference(x_words, x_scales, d_words, d_scales, gs, offs, k1, two, k2, n1, n2, n3, n4, n5, k3, k4, hz, n6, n7, n8, n9, n10):
    d_k3 = unpack_weight(d_words, d_scales)[np.arange(K)[:, None], runs(k3, K)]
    d_k1 = unpack_weight(d_words, d_scales)[np.arange(K)[:, None], runs(k1, K)]
    xq = unpack_weight(x_words, x_scales)[:, unstriped(offs)]
    d_k2 = unpack_weight(d_words, d_scales)[np.arange(K)[:, None], runs(k2, K)]
    x_two = unpack_weight(x_words, x_scales)[:, unstriped(two)]
    h = 0.0625 * (d_k1.T @ xq + d_k2.T @ x_two)
    pa = h[:, unstriped(n1)]
    pb = h[:, unstriped(n2)]
    rb = np.minimum(pa, pb)
    ra = pa - pb
    ua = np.zeros((H, S))
    ua[:, unstriped(n3)] = ra
    ub = ua.copy()
    ub[:, unstriped(n4)] = rb
    z = f64(gs) * (np.maximum(ub, ub[:, unstriped(n5)]))
    d_k4 = unpack_weight(d_words, d_scales)[np.arange(K)[:, None], runs(k4, K)]
    x_hz = unpack_weight(x_words, x_scales)[np.arange(K)[:, None], runs(hz, K)]
    h2 = 0.0625 * ((d_k3.T @ mxq(z, 0, "e4m3") + d_k4.T @ x_hz))
    pa2 = h2[:, unstriped(n6)]
    pb2 = h2[:, unstriped(n7)]
    rb2 = np.maximum(pa2, pb2)
    ua2 = np.zeros((H, S))
    ua2[:, unstriped(n8)] = pb2
    ub2 = ua2.copy()
    ub2[:, unstriped(n9)] = rb2
    out_0 = ub2 - h2[:, unstriped(n10)]
    return (out_0,) + planes(out_0)

@@ -1,0 +1,280 @@
+from contextlib import ExitStack
+
+import concourse.mybir as mybir
+
+F32 = mybir.dt.float32
+BF16 = mybir.dt.bfloat16
+I32 = mybir.dt.int32
+U32 = mybir.dt.uint32
+U16 = mybir.dt.uint16
+U8 = mybir.dt.uint8
+FP8X4 = mybir.dt.float8_e4m3fn_x4
+ALU = mybir.AluOpType
+COPY = mybir.ActivationFunctionType.Copy
+
+P = 128
+PACK = 4
+T, S, G, H, W = 1024, 256, 2048, 512, 128
+SPARE = 8
+ALIGN = 64
+FLOPS = 4 * 2 * 512 * H * S
+
+
+def tile_picked_mttzmhcpgfcpsw_none_po_kernel(
+    tc, x_words, x_scales, d_words, d_scales, gs, offs, k1, two, k2, n1, n2, n3, n4, n5,
+    k3, k4, hz, n6, n7, n8, n9, n10, out_0, out_1, out_2,
+):
+    nc = tc.nc
+    with ExitStack() as ctx:
+        held = ctx.enter_context(tc.tile_pool(name="held", bufs=1))
+        psum = ctx.enter_context(tc.psum_pool(name="psum", bufs=1))
+
+        def tile(name, shape, dtype, tag=None):
+            return held.tile(shape, dtype, name=name, tag=tag or name, align_bytes=ALIGN)
+
+        def load_list(name, src):
+            dst = held.tile(list(src.shape), U16, name=name)
+            nc.sync.dma_start(dst[:], src)
+            return dst
+
+        def load_scales(name, src, width):
+            dst = tile(name, [P, width], U8)
+            rows = src[0].bitcast(I32).unsqueeze(1).broadcast_to([16, 8, width // 4])
+            nc.sync.dma_start(out=dst[:].bitcast(I32), in_=rows)
+            return dst
+
+        def load_words(queue, name, src, width):
+            dst = tile(name, [P, width], U32)
+            queue.dma_start(out=dst[:].bitcast(I32), in_=src[0].rearrange("p n t -> p (n t)").bitcast(I32))
+            return dst
+
+        def gather(dst, window, offsets):
+            nc.vector.tensor_copy(out=dst, in_=window[:].indirect(offsets[:]))
+
+        def place_rows(queue, dst, src):
+            for c in range(PACK):
+                queue.dma_start(out=dst[c:P:32, :].bitcast(I32), in_=src[8 * c:P:32, :].bitcast(I32))
+
+        def deal_words(dst, src):
+            nc.vector.tensor_copy(
+                out=dst[:].bitcast(I32).rearrange("p (t m) -> p m t", t=PACK),
+                in_=src[:].bitcast(I32).rearrange("p (m t) -> p m t", t=PACK),
+            )
+
+        def deal_bytes(dst, src):
+            nc.vector.tensor_copy(
+                out=dst.rearrange("p (l t m) -> p l m t", m=P, t=PACK),
+                in_=src.rearrange("p (l m t) -> p l m t", m=P, t=PACK),
+            )
+
+        def move_bytes(dst, src):
+            nc.vector.tensor_copy(out=dst.bitcast(I32), in_=src.bitcast(I32))
+
+        def product(acc, words, scales, x, x_scale, t, start, stop):
+            cols = slice(t * P, (t + 1) * P)
+            nc.tensor.matmul_mx(
+                out=acc, lhsT=words[:, cols].bitcast(FP8X4), lhsT_scale=scales[:, cols],
+                rhs=x.bitcast(FP8X4), rhs_scale=x_scale, start=start, stop=stop,
+            )
+
+        def fetch(dst, window, offsets):
+            nc.scalar.activation(out=dst, in_=window[:].indirect(offsets), func=COPY)
+
+        def put(window, offsets, src):
+            nc.scalar.activation(out=window[:].indirect(offsets[:]), in_=src, func=COPY)
+
+        k1_t = load_list("k1_t", k1)
+        ds = load_scales("ds", d_scales, G)
+        k2_t = load_list("k2_t", k2)
+        xs = load_scales("xs", x_scales, T)
+        offs_t = load_list("offs_t", offs)
+        two_t = load_list("two_t", two)
+        dw = load_words(nc.sync, "dw", d_words, G)
+        xw = load_words(nc.gpsimd, "xw", x_words, T)
+        hz_t = load_list("hz_t", hz)
+        n1_t = load_list("n1_t", n1)
+        n2_t = load_list("n2_t", n2)
+        k3_t = load_list("k3_t", k3)
+        k4_t = load_list("k4_t", k4)
+        n3_t = load_list("n3_t", n3)
+        n4_t = load_list("n4_t", n4)
+        n5_t = load_list("n5_t", n5)
+        gs_t = tile("gs_t", [P, PACK], F32)
+        nc.gpsimd.dma_start(out=gs_t[:], in_=gs.rearrange("(p t) o -> p (t o)", t=PACK))
+        n7_t = load_list("n7_t", n7)
+        n6_t = load_list("n6_t", n6)
+        n8_t = load_list("n8_t", n8)
+        n9_t = load_list("n9_t", n9)
+        n10_t = load_list("n10_t", n10)
+
+        scales_1 = tile("scales_1", [P, 2 * H + 2 * S], U8)
+        scales_2 = tile("scales_2", [P, 2 * H + S], U8)
+        for dst in (scales_1, scales_2):
+            nc.vector.memset(dst[:].bitcast(I32), 0)
+        ub = [tile(f"ub{t}", [P, S + SPARE], F32) for t in range(PACK)]
+        ub2 = [tile(f"ub2{t}", [P, S + SPARE], F32) for t in range(PACK)]
+        h = [tile(f"h{t}", [P, S + SPARE], F32) for t in range(PACK)]
+        h2 = [tile(f"h2{t}", [P, S + SPARE], F32) for t in range(PACK)]
+        for t in range(PACK):
+            nc.vector.memset(ub[t][:], 0.0)
+        for t in range(PACK):
+            nc.gpsimd.memset(h2[t][:, S:], 0.0)
+            nc.gpsimd.memset(h[t][:, S:], 0.0)
+            nc.gpsimd.memset(ub2[t][:], 0.0)
+
+        bytes_1 = tile("bytes_1", [P, 2 * H + 2 * S], U8)
+        gather(bytes_1[:, :H], ds, k1_t)
+        gather(bytes_1[:, H:2 * H], ds, k2_t)
+        gather(bytes_1[:, 2 * H:2 * H + S], xs, offs_t)
+        gather(bytes_1[:, 2 * H + S:], xs, two_t)
+        dealt_1 = tile("dealt_1", [P, 2 * H + 2 * S], U8)
+        deal_bytes(dealt_1[:, :2 * H], bytes_1[:, :2 * H])
+        move_bytes(dealt_1[:, 2 * H:], bytes_1[:, 2 * H:])
+        place_rows(nc.scalar, scales_1, dealt_1)
+
+        words_k1 = tile("words_k1", [P, H], U32)
+        gather(words_k1[:], dw, k1_t)
+        words_k2 = tile("words_k2", [P, H], U32)
+        gather(words_k2[:], dw, k2_t)
+        dealt_k1 = tile("dealt_k1", [P, H], U32)
+        deal_words(dealt_k1, words_k1)
+        dealt_k2 = tile("dealt_k2", [P, H], U32)
+        deal_words(dealt_k2, words_k2)
+        words_offs = tile("words_offs", [P, S], U32)
+        gather(words_offs[:], xw, offs_t)
+        words_two = tile("words_two", [P, S], U32)
+        gather(words_two[:], xw, two_t)
+
+        acc = [psum.tile([P, S], F32, name=f"acc{t}") for t in range(PACK)]
+        for t in range(PACK):
+            product(acc[t][:], dealt_k1, scales_1[:, :H], words_offs[:], scales_1[:, 2 * H:2 * H + S], t, True, False)
+            product(acc[t][:], dealt_k2, scales_1[:, H:2 * H], words_two[:], scales_1[:, 2 * H + S:], t, False, True)
+
+        bytes_hz = tile("bytes_hz", [P, S], U8, tag="words_k2")
+        gather(bytes_hz[:], xs, hz_t)
+        nc.scalar.activation(out=h[0][:, :S], in_=acc[0][:], func=COPY, scale=0.0625)
+        for t in range(1, PACK):
+            nc.vector.tensor_scalar(out=h[t][:, :S], in0=acc[t][:], scalar1=0.0625, scalar2=None, op0=ALU.mult)
+
+        pairs = [tile(f"pairs{u}", [P, 2, 2, W], F32) for u in range(2)]
+        mixed = [tile(f"mixed{u}", [P, 2, 2, W], F32) for u in range(2)]
+        for t in range(PACK):
+            fetch(pairs[t // 2][:, 0, t % 2, :], h[t], n1_t[:])
+            fetch(pairs[t // 2][:, 1, t % 2, :], h[t], n2_t[:])
+
+        def mix(u):
+            nc.vector.tensor_tensor(out=mixed[u][:, 0], in0=pairs[u][:, 0], in1=pairs[u][:, 1], op=ALU.subtract)
+            nc.vector.tensor_tensor(out=mixed[u][:, 1], in0=pairs[u][:, 0], in1=pairs[u][:, 1], op=ALU.min)
+
+        z_bf = tile("z_bf", [P, S, PACK], BF16)
+        far = [tile(f"far{t}", [P, S], F32) for t in range(PACK)]
+        top = [tile(f"top{t}", [P, S], F32) for t in range(PACK)]
+
+        def put_a(t):
+            put(ub[t], n3_t, mixed[t // 2][:, 0, t % 2, :])
+
+        def put_b(t):
+            put(ub[t], n4_t, mixed[t // 2][:, 1, t % 2, :])
+
+        def close(t):
+            fetch(far[t][:], ub[t], n5_t[:])
+            nc.vector.tensor_tensor(out=top[t][:], in0=ub[t][:, :S], in1=far[t][:], op=ALU.max)
+            nc.vector.tensor_scalar(out=z_bf[:, :, t], in0=top[t][:], scalar1=gs_t[:, t:t + 1], scalar2=None, op0=ALU.mult)
+
+        mix(0)
+        bytes_k3 = tile("bytes_k3", [P, H], U8, tag="pairs0")
+        gather(bytes_k3[:], ds, k3_t)
+        mix(1)
+        bytes_k4 = tile("bytes_k4", [P, H], U8, tag="pairs1")
+        gather(bytes_k4[:], ds, k4_t)
+        dealt_2 = tile("dealt_2", [P, 2 * H + S], U8)
+        move_bytes(dealt_2[:, 2 * H:], bytes_hz[:])
+        deal_bytes(dealt_2[:, :H], bytes_k3[:])
+        deal_bytes(dealt_2[:, H:2 * H], bytes_k4[:])
+        place_rows(nc.sync, scales_2, dealt_2)
+        words_k3 = tile("words_k3", [P, H], U32, tag="pairs1")
+        gather(words_k3[:], dw, k3_t)
+        put_a(0)
+        put_a(1)
+        put_b(0)
+        put_b(1)
+        close(0)
+        dealt_k3 = tile("dealt_k3", [P, H], U32)
+        deal_words(dealt_k3, words_k3)
+        words_k4 = tile("words_k4", [P, H], U32, tag="far0")
+        gather(words_k4[:], dw, k4_t)
+        put_a(2)
+        close(1)
+        dealt_k4 = tile("dealt_k4", [P, H], U32)
+        deal_words(dealt_k4, words_k4)
+        words_hz = tile("words_hz", [P, S], U32, tag="far1")
+        gather(words_hz[:], xw, hz_t)
+        acc2 = [psum.tile([P, S], F32, name=f"acc2{t}") for t in range(PACK)]
+        for t in range(PACK):
+            product(acc2[t][:], dealt_k4, scales_2[:, H:2 * H], words_hz[:], scales_2[:, 2 * H:], t, True, False)
+        put_b(2)
+        put_a(3)
+        close(2)
+        put_b(3)
+        halves = [slice(0, W), slice(W, S)]
+        list_halves = [slice(0, W // 16), slice(W // 16, S // 16)]
+        last = PACK - 1
+        for cols, entries in zip(halves, list_halves):
+            fetch(far[last][:, cols], ub[last], n5_t[:, entries])
+            nc.vector.tensor_tensor(out=top[last][:, cols], in0=ub[last][:, cols], in1=far[last][:, cols], op=ALU.max)
+        for cols in halves:
+            nc.vector.tensor_scalar(out=z_bf[:, cols, last], in0=top[last][:, cols], scalar1=gs_t[:, last:], scalar2=None, op0=ALU.mult)
+
+        z_words = tile("z_words", [P, S], U32)
+        z_scales = tile("z_scales", [P, S], U8)
+        for cols in halves:
+            nc.vector.quantize_mx(out=z_words[:, cols].bitcast(FP8X4), scales=z_scales[:, cols], in_=z_bf[:, cols, :].rearrange("p j t -> p (j t)"))
+        for t in range(PACK):
+            for cols in halves:
+                product(acc2[t][:, cols], dealt_k3, scales_2[:, :H], z_words[:, cols], z_scales[:, cols], t, False, cols == halves[1])
+        nc.scalar.activation(out=h2[0][:, :S], in_=acc2[0][:], func=COPY, scale=0.0625)
+        for t in range(1, PACK):
+            nc.vector.tensor_scalar(out=h2[t][:, :S], in0=acc2[t][:], scalar1=0.0625, scalar2=None, op0=ALU.mult)
+
+        pairs2 = [tile(f"pairs2{u}", [P, 2, 2, W], F32) for u in range(2)]
+        larger = [tile(f"larger{u}", [P, 2, W], F32) for u in range(2)]
+        far2 = [tile(f"far2{t}", [P, S], F32) for t in range(PACK)]
+        res = [tile(f"res{t}", [P, S], F32) for t in range(PACK)]
+        res_bf = tile("res_bf", [P, S, PACK], BF16)
+        out_rows = out_0.rearrange("(p t) j -> p t j", t=PACK)
+
+        def finish(t):
+            nc.vector.tensor_tensor(out=res[t][:], in0=ub2[t][:, :S], in1=far2[t][:], op=ALU.subtract)
+            nc.sync.dma_start(out=out_rows[:, t, :], in_=res[t][:])
+            nc.vector.tensor_copy(out=res_bf[:, :, t], in_=res[t][:])
+
+        for u in range(2):
+            t0, t1 = 2 * u, 2 * u + 1
+            for v in range(2):
+                fetch(pairs2[u][:, 1, v, :], h2[t0 + v], n7_t[:])
+                fetch(pairs2[u][:, 0, v, :], h2[t0 + v], n6_t[:])
+            nc.vector.tensor_tensor(out=larger[u][:], in0=pairs2[u][:, 0], in1=pairs2[u][:, 1], op=ALU.max)
+            put(ub2[t0], n8_t, pairs2[u][:, 1, 0, :])
+            put(ub2[t1], n8_t, pairs2[u][:, 1, 1, :])
+            put(ub2[t0], n9_t, larger[u][:, 0, :])
+            fetch(far2[t0][:], h2[t0], n10_t[:])
+            finish(t0)
+            put(ub2[t1], n9_t, larger[u][:, 1, :])
+            if t1 != last:
+                fetch(far2[t1][:], h2[t1], n10_t[:])
+                finish(t1)
+
+        for cols, entries in zip(halves, list_halves):
+            fetch(far2[last][:, cols], h2[last], n10_t[:, entries])
+            nc.vector.tensor_tensor(out=res[last][:, cols], in0=ub2[last][:, cols], in1=far2[last][:, cols], op=ALU.subtract)
+        nc.sync.dma_start(out=out_rows[:, last, :], in_=res[last][:])
+        for cols in halves:
+            nc.vector.tensor_copy(out=res_bf[:, cols, last], in_=res[last][:, cols])
+        res_words = tile("res_words", [P, S], U32)
+        res_scales = tile("res_scales", [P, S], U8)
+        for cols in halves:
+            nc.vector.quantize_mx(out=res_words[:, cols].bitcast(FP8X4), scales=res_scales[:, cols], in_=res_bf[:, cols, :].rearrange("p j t -> p (j t)"))
+        nc.sync.dma_start(out=out_1[0].rearrange("p c r -> p (c r)").bitcast(I32), in_=res_words[:].bitcast(I32))
+        for q in range(4):
+            queue = nc.scalar if q % 2 == 0 else nc.sync
+            queue.dma_start(out=out_2[0, 4 * q:4 * q + 4, :].bitcast(I32), in_=res_scales[32 * q:32 * q + 4, :].bitcast(I32))

@@ -83,24 +83,24 @@ def tile_picked_mttzmhcpgfcpsw_none_po_kernel(
         def put(window, offsets, src):
             nc.scalar.activation(out=window[:].indirect(offsets[:]), in_=src, func=COPY)
 
-        k1_t = load_list("k1_t", k1)
-        ds = load_scales("ds", d_scales, G)
-        k2_t = load_list("k2_t", k2)
-        xs = load_scales("xs", x_scales, T)
         offs_t = load_list("offs_t", offs)
+        xs = load_scales("xs", x_scales, T)
+        ds = load_scales("ds", d_scales, G)
+        k1_t = load_list("k1_t", k1)
+        k2_t = load_list("k2_t", k2)
         two_t = load_list("two_t", two)
-        dw = load_words(nc.sync, "dw", d_words, G)
-        xw = load_words(nc.gpsimd, "xw", x_words, T)
-        hz_t = load_list("hz_t", hz)
+        k3_t = load_list("k3_t", k3)
         n1_t = load_list("n1_t", n1)
         n2_t = load_list("n2_t", n2)
-        k3_t = load_list("k3_t", k3)
+        hz_t = load_list("hz_t", hz)
+        dw = load_words(nc.sync, "dw", d_words, G)
+        xw = load_words(nc.sync, "xw", x_words, T)
         k4_t = load_list("k4_t", k4)
         n3_t = load_list("n3_t", n3)
         n4_t = load_list("n4_t", n4)
         n5_t = load_list("n5_t", n5)
         gs_t = tile("gs_t", [P, PACK], F32)
-        nc.gpsimd.dma_start(out=gs_t[:], in_=gs.rearrange("(p t) o -> p (t o)", t=PACK))
+        nc.sync.dma_start(out=gs_t[:], in_=gs.rearrange("(p t) o -> p (t o)", t=PACK))
         n7_t = load_list("n7_t", n7)
         n6_t = load_list("n6_t", n6)
         n8_t = load_list("n8_t", n8)
@@ -115,17 +115,13 @@ def tile_picked_mttzmhcpgfcpsw_none_po_kernel(
         ub2 = [tile(f"ub2{t}", [P, S + SPARE], F32) for t in range(PACK)]
         h = [tile(f"h{t}", [P, S + SPARE], F32) for t in range(PACK)]
         h2 = [tile(f"h2{t}", [P, S + SPARE], F32) for t in range(PACK)]
-        for t in range(PACK):
-            nc.vector.memset(ub[t][:], 0.0)
-        for t in range(PACK):
-            nc.gpsimd.memset(h2[t][:, S:], 0.0)
-            nc.gpsimd.memset(h[t][:, S:], 0.0)
-            nc.gpsimd.memset(ub2[t][:], 0.0)
+        for window in h + ub + h2 + ub2:
+            nc.vector.memset(window[:, S:], 0.0)
 
         bytes_1 = tile("bytes_1", [P, 2 * H + 2 * S], U8)
+        gather(bytes_1[:, 2 * H:2 * H + S], xs, offs_t)
         gather(bytes_1[:, :H], ds, k1_t)
         gather(bytes_1[:, H:2 * H], ds, k2_t)
-        gather(bytes_1[:, 2 * H:2 * H + S], xs, offs_t)
         gather(bytes_1[:, 2 * H + S:], xs, two_t)
         dealt_1 = tile("dealt_1", [P, 2 * H + 2 * S], U8)
         deal_bytes(dealt_1[:, :2 * H], bytes_1[:, :2 * H])
@@ -134,31 +130,34 @@ def tile_picked_mttzmhcpgfcpsw_none_po_kernel(
 
         words_k1 = tile("words_k1", [P, H], U32)
         gather(words_k1[:], dw, k1_t)
-        words_k2 = tile("words_k2", [P, H], U32)
-        gather(words_k2[:], dw, k2_t)
-        dealt_k1 = tile("dealt_k1", [P, H], U32)
-        deal_words(dealt_k1, words_k1)
-        dealt_k2 = tile("dealt_k2", [P, H], U32)
-        deal_words(dealt_k2, words_k2)
         words_offs = tile("words_offs", [P, S], U32)
         gather(words_offs[:], xw, offs_t)
+        dealt_k1 = tile("dealt_k1", [P, H], U32)
+        deal_words(dealt_k1, words_k1)
+        words_k2 = tile("words_k2", [P, H], U32)
+        gather(words_k2[:], dw, k2_t)
         words_two = tile("words_two", [P, S], U32)
         gather(words_two[:], xw, two_t)
+        dealt_k2 = tile("dealt_k2", [P, H], U32)
+        deal_words(dealt_k2, words_k2)
 
         acc = [psum.tile([P, S], F32, name=f"acc{t}") for t in range(PACK)]
         for t in range(PACK):
             product(acc[t][:], dealt_k1, scales_1[:, :H], words_offs[:], scales_1[:, 2 * H:2 * H + S], t, True, False)
             product(acc[t][:], dealt_k2, scales_1[:, H:2 * H], words_two[:], scales_1[:, 2 * H + S:], t, False, True)
 
-        bytes_hz = tile("bytes_hz", [P, S], U8, tag="words_k2")
-        gather(bytes_hz[:], xs, hz_t)
-        nc.scalar.activation(out=h[0][:, :S], in_=acc[0][:], func=COPY, scale=0.0625)
-        for t in range(1, PACK):
+        bytes_k3 = tile("bytes_k3", [P, H], U8, tag="words_k2")
+        gather(bytes_k3[:], ds, k3_t)
+        for t in range(2, PACK):
             nc.vector.tensor_scalar(out=h[t][:, :S], in0=acc[t][:], scalar1=0.0625, scalar2=None, op0=ALU.mult)
+        bytes_hz = tile("bytes_hz", [P, S], U8, tag="words_two")
+        gather(bytes_hz[:], xs, hz_t)
 
         pairs = [tile(f"pairs{u}", [P, 2, 2, W], F32) for u in range(2)]
         mixed = [tile(f"mixed{u}", [P, 2, 2, W], F32) for u in range(2)]
         for t in range(PACK):
+            if t < 2:
+                nc.scalar.activation(out=h[t][:, :S], in_=acc[t][:], func=COPY, scale=0.0625)
             fetch(pairs[t // 2][:, 0, t % 2, :], h[t], n1_t[:])
             fetch(pairs[t // 2][:, 1, t % 2, :], h[t], n2_t[:])
 
@@ -168,7 +167,6 @@ def tile_picked_mttzmhcpgfcpsw_none_po_kernel(
 
         z_bf = tile("z_bf", [P, S, PACK], BF16)
         far = [tile(f"far{t}", [P, S], F32) for t in range(PACK)]
-        top = [tile(f"top{t}", [P, S], F32) for t in range(PACK)]
 
         def put_a(t):
             put(ub[t], n3_t, mixed[t // 2][:, 0, t % 2, :])
@@ -176,54 +174,63 @@ def tile_picked_mttzmhcpgfcpsw_none_po_kernel(
         def put_b(t):
             put(ub[t], n4_t, mixed[t // 2][:, 1, t % 2, :])
 
-        def close(t):
-            fetch(far[t][:], ub[t], n5_t[:])
-            nc.vector.tensor_tensor(out=top[t][:], in0=ub[t][:, :S], in1=far[t][:], op=ALU.max)
-            nc.vector.tensor_scalar(out=z_bf[:, :, t], in0=top[t][:], scalar1=gs_t[:, t:t + 1], scalar2=None, op0=ALU.mult)
-
         mix(0)
-        bytes_k3 = tile("bytes_k3", [P, H], U8, tag="pairs0")
-        gather(bytes_k3[:], ds, k3_t)
-        mix(1)
-        bytes_k4 = tile("bytes_k4", [P, H], U8, tag="pairs1")
-        gather(bytes_k4[:], ds, k4_t)
         dealt_2 = tile("dealt_2", [P, 2 * H + S], U8)
-        move_bytes(dealt_2[:, 2 * H:], bytes_hz[:])
         deal_bytes(dealt_2[:, :H], bytes_k3[:])
+        bytes_k4 = tile("bytes_k4", [P, H], U8, tag="pairs0")
+        gather(bytes_k4[:], ds, k4_t)
+        mix(1)
+        move_bytes(dealt_2[:, 2 * H:], bytes_hz[:])
         deal_bytes(dealt_2[:, H:2 * H], bytes_k4[:])
         place_rows(nc.sync, scales_2, dealt_2)
         words_k3 = tile("words_k3", [P, H], U32, tag="pairs1")
         gather(words_k3[:], dw, k3_t)
-        put_a(0)
-        put_a(1)
-        put_b(0)
-        put_b(1)
-        close(0)
+        words_k4 = tile("words_k4", [P, H], U32, tag="pairs0")
+        gather(words_k4[:], dw, k4_t)
         dealt_k3 = tile("dealt_k3", [P, H], U32)
         deal_words(dealt_k3, words_k3)
-        words_k4 = tile("words_k4", [P, H], U32, tag="far0")
-        gather(words_k4[:], dw, k4_t)
-        put_a(2)
-        close(1)
         dealt_k4 = tile("dealt_k4", [P, H], U32)
         deal_words(dealt_k4, words_k4)
-        words_hz = tile("words_hz", [P, S], U32, tag="far1")
+        words_hz = tile("words_hz", [P, S], U32, tag="pairs1")
         gather(words_hz[:], xw, hz_t)
         acc2 = [psum.tile([P, S], F32, name=f"acc2{t}") for t in range(PACK)]
         for t in range(PACK):
             product(acc2[t][:], dealt_k4, scales_2[:, H:2 * H], words_hz[:], scales_2[:, 2 * H:], t, True, False)
+
+        top = tile("top", [P, PACK, S], F32, tag="pairs0")
+
+        def larger_of(t, cols):
+            nc.vector.tensor_tensor(out=top[:, t, cols], in0=ub[t][:, cols], in1=far[t][:, cols], op=ALU.max)
+
+        def weigh(t, cols):
+            nc.vector.tensor_scalar(out=z_bf[:, cols, t], in0=top[:, t, cols], scalar1=gs_t[:, t:t + 1], scalar2=None, op0=ALU.mult)
+
+        whole = slice(0, S)
+        put_a(0)
+        put_a(1)
+        put_b(0)
+        put_b(1)
+        fetch(far[0][:], ub[0], n5_t[:])
+        put_a(2)
+        fetch(far[1][:], ub[1], n5_t[:])
+        for t in range(2):
+            larger_of(t, whole)
+        for t in range(2):
+            weigh(t, whole)
         put_b(2)
         put_a(3)
-        close(2)
+        fetch(far[2][:], ub[2], n5_t[:])
+        larger_of(2, whole)
+        weigh(2, whole)
         put_b(3)
         halves = [slice(0, W), slice(W, S)]
         list_halves = [slice(0, W // 16), slice(W // 16, S // 16)]
         last = PACK - 1
         for cols, entries in zip(halves, list_halves):
             fetch(far[last][:, cols], ub[last], n5_t[:, entries])
-            nc.vector.tensor_tensor(out=top[last][:, cols], in0=ub[last][:, cols], in1=far[last][:, cols], op=ALU.max)
+            larger_of(last, cols)
         for cols in halves:
-            nc.vector.tensor_scalar(out=z_bf[:, cols, last], in0=top[last][:, cols], scalar1=gs_t[:, last:], scalar2=None, op0=ALU.mult)
+            weigh(last, cols)
 
         z_words = tile("z_words", [P, S], U32)
         z_scales = tile("z_scales", [P, S], U8)

@@ -142,9 +142,11 @@ def tile_picked_mttzmhcpgfcpsw_none_po_kernel(
         deal_words(dealt_k2, words_k2)
 
         acc = [psum.tile([P, S], F32, name=f"acc{t}") for t in range(PACK)]
-        for t in range(PACK):
-            product(acc[t][:], dealt_k1, scales_1[:, :H], words_offs[:], scales_1[:, 2 * H:2 * H + S], t, True, False)
-            product(acc[t][:], dealt_k2, scales_1[:, H:2 * H], words_two[:], scales_1[:, 2 * H + S:], t, False, True)
+        for group in ((0, 1), (2,), (3,)):
+            for t in group:
+                product(acc[t][:], dealt_k1, scales_1[:, :H], words_offs[:], scales_1[:, 2 * H:2 * H + S], t, True, False)
+            for t in group:
+                product(acc[t][:], dealt_k2, scales_1[:, H:2 * H], words_two[:], scales_1[:, 2 * H + S:], t, False, True)
 
         bytes_k3 = tile("bytes_k3", [P, H], U8, tag="words_k2")
         gather(bytes_k3[:], ds, k3_t)
@@ -237,15 +239,14 @@ def tile_picked_mttzmhcpgfcpsw_none_po_kernel(
         for cols in halves:
             nc.vector.quantize_mx(out=z_words[:, cols].bitcast(FP8X4), scales=z_scales[:, cols], in_=z_bf[:, cols, :].rearrange("p j t -> p (j t)"))
         for t in range(PACK):
-            for cols in halves:
-                product(acc2[t][:, cols], dealt_k3, scales_2[:, :H], z_words[:, cols], z_scales[:, cols], t, False, cols == halves[1])
+            product(acc2[t][:], dealt_k3, scales_2[:, :H], z_words[:], z_scales[:], t, False, True)
         nc.scalar.activation(out=h2[0][:, :S], in_=acc2[0][:], func=COPY, scale=0.0625)
         for t in range(1, PACK):
             nc.vector.tensor_scalar(out=h2[t][:, :S], in0=acc2[t][:], scalar1=0.0625, scalar2=None, op0=ALU.mult)
 
         pairs2 = [tile(f"pairs2{u}", [P, 2, 2, W], F32) for u in range(2)]
         larger = [tile(f"larger{u}", [P, 2, W], F32) for u in range(2)]
-        far2 = [tile(f"far2{t}", [P, S], F32) for t in range(PACK)]
+        far2 = [tile(f"far2{t}", [P, S], F32) for t in range(2)]
         res = [tile(f"res{t}", [P, S], F32) for t in range(PACK)]
         res_bf = tile("res_bf", [P, S, PACK], BF16)
         out_rows = out_0.rearrange("(p t) j -> p t j", t=PACK)
@@ -264,6 +265,9 @@ def tile_picked_mttzmhcpgfcpsw_none_po_kernel(
             put(ub2[t0], n8_t, pairs2[u][:, 1, 0, :])
             put(ub2[t1], n8_t, pairs2[u][:, 1, 1, :])
             put(ub2[t0], n9_t, larger[u][:, 0, :])
+            if u == 1:
+                far2.append(tile("far22", [P, S], F32, tag="larger0"))
+                far2.append(tile("far23", [P, S], F32, tag="pairs21"))
             fetch(far2[t0][:], h2[t0], n10_t[:])
             finish(t0)
             put(ub2[t1], n9_t, larger[u][:, 1, :])

from contextlib import ExitStack

import concourse.mybir as mybir

F32 = mybir.dt.float32
BF16 = mybir.dt.bfloat16
I32 = mybir.dt.int32
U32 = mybir.dt.uint32
U16 = mybir.dt.uint16
U8 = mybir.dt.uint8
FP8X4 = mybir.dt.float8_e4m3fn_x4
ALU = mybir.AluOpType
COPY = mybir.ActivationFunctionType.Copy

P = 128
PACK = 4
T, S, G, H, W = 1024, 256, 2048, 512, 128
SPARE = 8
ALIGN = 64
FLOPS = 4 * 2 * 512 * H * S


def tile_picked_mttzmhcpgfcpsw_none_po_kernel(
    tc, x_words, x_scales, d_words, d_scales, gs, offs, k1, two, k2, n1, n2, n3, n4, n5,
    k3, k4, hz, n6, n7, n8, n9, n10, out_0, out_1, out_2,
):
    nc = tc.nc
    with ExitStack() as ctx:
        held = ctx.enter_context(tc.tile_pool(name="held", bufs=1))
        psum = ctx.enter_context(tc.psum_pool(name="psum", bufs=1))

        def tile(name, shape, dtype, tag=None):
            return held.tile(shape, dtype, name=name, tag=tag or name, align_bytes=ALIGN)

        def load_list(name, src):
            dst = held.tile(list(src.shape), U16, name=name)
            nc.sync.dma_start(dst[:], src)
            return dst

        def load_scales(name, src, width):
            dst = tile(name, [P, width], U8)
            rows = src[0].bitcast(I32).unsqueeze(1).broadcast_to([16, 8, width // 4])
            nc.sync.dma_start(out=dst[:].bitcast(I32), in_=rows)
            return dst

        def load_words(queue, name, src, width):
            dst = tile(name, [P, width], U32)
            queue.dma_start(out=dst[:].bitcast(I32), in_=src[0].rearrange("p n t -> p (n t)").bitcast(I32))
            return dst

        def gather(dst, window, offsets):
            nc.vector.tensor_copy(out=dst, in_=window[:].indirect(offsets[:]))

        def place_rows(queue, dst, src):
            for c in range(PACK):
                queue.dma_start(out=dst[c:P:32, :].bitcast(I32), in_=src[8 * c:P:32, :].bitcast(I32))

        def deal_words(dst, src):
            nc.vector.tensor_copy(
                out=dst[:].bitcast(I32).rearrange("p (t m) -> p m t", t=PACK),
                in_=src[:].bitcast(I32).rearrange("p (m t) -> p m t", t=PACK),
            )

        def deal_bytes(dst, src):
            nc.vector.tensor_copy(
                out=dst.rearrange("p (l t m) -> p l m t", m=P, t=PACK),
                in_=src.rearrange("p (l m t) -> p l m t", m=P, t=PACK),
            )

        def move_bytes(dst, src):
            nc.vector.tensor_copy(out=dst.bitcast(I32), in_=src.bitcast(I32))

        def product(acc, words, scales, x, x_scale, t, start, stop):
            cols = slice(t * P, (t + 1) * P)
            nc.tensor.matmul_mx(
                out=acc, lhsT=words[:, cols].bitcast(FP8X4), lhsT_scale=scales[:, cols],
                rhs=x.bitcast(FP8X4), rhs_scale=x_scale, start=start, stop=stop,
            )

        def fetch(dst, window, offsets):
            nc.scalar.activation(out=dst, in_=window[:].indirect(offsets), func=COPY)

        def put(window, offsets, src):
            nc.scalar.activation(out=window[:].indirect(offsets[:]), in_=src, func=COPY)

        offs_t = load_list("offs_t", offs)
        xs = load_scales("xs", x_scales, T)
        ds = load_scales("ds", d_scales, G)
        k1_t = load_list("k1_t", k1)
        k2_t = load_list("k2_t", k2)
        two_t = load_list("two_t", two)
        k3_t = load_list("k3_t", k3)
        n1_t = load_list("n1_t", n1)
        n2_t = load_list("n2_t", n2)
        hz_t = load_list("hz_t", hz)
        dw = load_words(nc.sync, "dw", d_words, G)
        xw = load_words(nc.sync, "xw", x_words, T)
        k4_t = load_list("k4_t", k4)
        n3_t = load_list("n3_t", n3)
        n4_t = load_list("n4_t", n4)
        n5_t = load_list("n5_t", n5)
        gs_t = tile("gs_t", [P, PACK], F32)
        nc.sync.dma_start(out=gs_t[:], in_=gs.rearrange("(p t) o -> p (t o)", t=PACK))
        n7_t = load_list("n7_t", n7)
        n6_t = load_list("n6_t", n6)
        n8_t = load_list("n8_t", n8)
        n9_t = load_list("n9_t", n9)
        n10_t = load_list("n10_t", n10)

        scales_1 = tile("scales_1", [P, 2 * H + 2 * S], U8)
        scales_2 = tile("scales_2", [P, 2 * H + S], U8)
        for dst in (scales_1, scales_2):
            nc.vector.memset(dst[:].bitcast(I32), 0)
        ub = [tile(f"ub{t}", [P, S + SPARE], F32) for t in range(PACK)]
        ub2 = [tile(f"ub2{t}", [P, S + SPARE], F32) for t in range(PACK)]
        h = [tile(f"h{t}", [P, S + SPARE], F32) for t in range(PACK)]
        h2 = [tile(f"h2{t}", [P, S + SPARE], F32) for t in range(PACK)]
        for window in h + ub + h2 + ub2:
            nc.vector.memset(window[:, S:], 0.0)

        bytes_1 = tile("bytes_1", [P, 2 * H + 2 * S], U8)
        gather(bytes_1[:, 2 * H:2 * H + S], xs, offs_t)
        gather(bytes_1[:, :H], ds, k1_t)
        gather(bytes_1[:, H:2 * H], ds, k2_t)
        gather(bytes_1[:, 2 * H + S:], xs, two_t)
        dealt_1 = tile("dealt_1", [P, 2 * H + 2 * S], U8)
        deal_bytes(dealt_1[:, :2 * H], bytes_1[:, :2 * H])
        move_bytes(dealt_1[:, 2 * H:], bytes_1[:, 2 * H:])
        place_rows(nc.scalar, scales_1, dealt_1)

        words_k1 = tile("words_k1", [P, H], U32)
        gather(words_k1[:], dw, k1_t)
        words_offs = tile("words_offs", [P, S], U32)
        gather(words_offs[:], xw, offs_t)
        dealt_k1 = tile("dealt_k1", [P, H], U32)
        deal_words(dealt_k1, words_k1)
        words_k2 = tile("words_k2", [P, H], U32)
        gather(words_k2[:], dw, k2_t)
        words_two = tile("words_two", [P, S], U32)
        gather(words_two[:], xw, two_t)
        dealt_k2 = tile("dealt_k2", [P, H], U32)
        deal_words(dealt_k2, words_k2)

        acc = [psum.tile([P, S], F32, name=f"acc{t}") for t in range(PACK)]
        for group in ((0, 1), (2,), (3,)):
            for t in group:
                product(acc[t][:], dealt_k1, scales_1[:, :H], words_offs[:], scales_1[:, 2 * H:2 * H + S], t, True, False)
            for t in group:
                product(acc[t][:], dealt_k2, scales_1[:, H:2 * H], words_two[:], scales_1[:, 2 * H + S:], t, False, True)

        bytes_k3 = tile("bytes_k3", [P, H], U8, tag="words_k2")
        gather(bytes_k3[:], ds, k3_t)
        for t in range(2, PACK):
            nc.vector.tensor_scalar(out=h[t][:, :S], in0=acc[t][:], scalar1=0.0625, scalar2=None, op0=ALU.mult)
        bytes_hz = tile("bytes_hz", [P, S], U8, tag="words_two")
        gather(bytes_hz[:], xs, hz_t)

        pairs = [tile(f"pairs{u}", [P, 2, 2, W], F32) for u in range(2)]
        mixed = [tile(f"mixed{u}", [P, 2, 2, W], F32) for u in range(2)]
        for t in range(PACK):
            if t < 2:
                nc.scalar.activation(out=h[t][:, :S], in_=acc[t][:], func=COPY, scale=0.0625)
            fetch(pairs[t // 2][:, 0, t % 2, :], h[t], n1_t[:])
            fetch(pairs[t // 2][:, 1, t % 2, :], h[t], n2_t[:])

        def mix(u):
            nc.vector.tensor_tensor(out=mixed[u][:, 0], in0=pairs[u][:, 0], in1=pairs[u][:, 1], op=ALU.subtract)
            nc.vector.tensor_tensor(out=mixed[u][:, 1], in0=pairs[u][:, 0], in1=pairs[u][:, 1], op=ALU.min)

        z_bf = tile("z_bf", [P, S, PACK], BF16)
        far = [tile(f"far{t}", [P, S], F32) for t in range(PACK)]

        def put_a(t):
            put(ub[t], n3_t, mixed[t // 2][:, 0, t % 2, :])

        def put_b(t):
            put(ub[t], n4_t, mixed[t // 2][:, 1, t % 2, :])

        mix(0)
        dealt_2 = tile("dealt_2", [P, 2 * H + S], U8)
        deal_bytes(dealt_2[:, :H], bytes_k3[:])
        bytes_k4 = tile("bytes_k4", [P, H], U8, tag="pairs0")
        gather(bytes_k4[:], ds, k4_t)
        mix(1)
        move_bytes(dealt_2[:, 2 * H:], bytes_hz[:])
        deal_bytes(dealt_2[:, H:2 * H], bytes_k4[:])
        place_rows(nc.sync, scales_2, dealt_2)
        words_k3 = tile("words_k3", [P, H], U32, tag="pairs1")
        gather(words_k3[:], dw, k3_t)
        words_k4 = tile("words_k4", [P, H], U32, tag="pairs0")
        gather(words_k4[:], dw, k4_t)
        dealt_k3 = tile("dealt_k3", [P, H], U32)
        deal_words(dealt_k3, words_k3)
        dealt_k4 = tile("dealt_k4", [P, H], U32)
        deal_words(dealt_k4, words_k4)
        words_hz = tile("words_hz", [P, S], U32, tag="pairs1")
        gather(words_hz[:], xw, hz_t)
        acc2 = [psum.tile([P, S], F32, name=f"acc2{t}") for t in range(PACK)]
        for t in range(PACK):
            product(acc2[t][:], dealt_k4, scales_2[:, H:2 * H], words_hz[:], scales_2[:, 2 * H:], t, True, False)

        top = tile("top", [P, PACK, S], F32, tag="pairs0")

        def larger_of(t, cols):
            nc.vector.tensor_tensor(out=top[:, t, cols], in0=ub[t][:, cols], in1=far[t][:, cols], op=ALU.max)

        def weigh(t, cols):
            nc.vector.tensor_scalar(out=z_bf[:, cols, t], in0=top[:, t, cols], scalar1=gs_t[:, t:t + 1], scalar2=None, op0=ALU.mult)

        whole = slice(0, S)
        put_a(0)
        put_a(1)
        put_b(0)
        put_b(1)
        fetch(far[0][:], ub[0], n5_t[:])
        put_a(2)
        fetch(far[1][:], ub[1], n5_t[:])
        for t in range(2):
            larger_of(t, whole)
        for t in range(2):
            weigh(t, whole)
        put_b(2)
        put_a(3)
        fetch(far[2][:], ub[2], n5_t[:])
        larger_of(2, whole)
        weigh(2, whole)
        put_b(3)
        halves = [slice(0, W), slice(W, S)]
        list_halves = [slice(0, W // 16), slice(W // 16, S // 16)]
        last = PACK - 1
        for cols, entries in zip(halves, list_halves):
            fetch(far[last][:, cols], ub[last], n5_t[:, entries])
            larger_of(last, cols)
        for cols in halves:
            weigh(last, cols)

        z_words = tile("z_words", [P, S], U32)
        z_scales = tile("z_scales", [P, S], U8)
        for cols in halves:
            nc.vector.quantize_mx(out=z_words[:, cols].bitcast(FP8X4), scales=z_scales[:, cols], in_=z_bf[:, cols, :].rearrange("p j t -> p (j t)"))
        for t in range(PACK):
            product(acc2[t][:], dealt_k3, scales_2[:, :H], z_words[:], z_scales[:], t, False, True)
        nc.scalar.activation(out=h2[0][:, :S], in_=acc2[0][:], func=COPY, scale=0.0625)
        for t in range(1, PACK):
            nc.vector.tensor_scalar(out=h2[t][:, :S], in0=acc2[t][:], scalar1=0.0625, scalar2=None, op0=ALU.mult)

        pairs2 = [tile(f"pairs2{u}", [P, 2, 2, W], F32) for u in range(2)]
        larger = [tile(f"larger{u}", [P, 2, W], F32) for u in range(2)]
        far2 = [tile(f"far2{t}", [P, S], F32) for t in range(2)]
        res = [tile(f"res{t}", [P, S], F32) for t in range(PACK)]
        res_bf = tile("res_bf", [P, S, PACK], BF16)
        out_rows = out_0.rearrange("(p t) j -> p t j", t=PACK)

        def finish(t):
            nc.vector.tensor_tensor(out=res[t][:], in0=ub2[t][:, :S], in1=far2[t][:], op=ALU.subtract)
            nc.sync.dma_start(out=out_rows[:, t, :], in_=res[t][:])
            nc.vector.tensor_copy(out=res_bf[:, :, t], in_=res[t][:])

        for u in range(2):
            t0, t1 = 2 * u, 2 * u + 1
            for v in range(2):
                fetch(pairs2[u][:, 1, v, :], h2[t0 + v], n7_t[:])
                fetch(pairs2[u][:, 0, v, :], h2[t0 + v], n6_t[:])
            nc.vector.tensor_tensor(out=larger[u][:], in0=pairs2[u][:, 0], in1=pairs2[u][:, 1], op=ALU.max)
            put(ub2[t0], n8_t, pairs2[u][:, 1, 0, :])
            put(ub2[t1], n8_t, pairs2[u][:, 1, 1, :])
            put(ub2[t0], n9_t, larger[u][:, 0, :])
            if u == 1:
                far2.append(tile("far22", [P, S], F32, tag="larger0"))
                far2.append(tile("far23", [P, S], F32, tag="pairs21"))
            fetch(far2[t0][:], h2[t0], n10_t[:])
            finish(t0)
            put(ub2[t1], n9_t, larger[u][:, 1, :])
            if t1 != last:
                fetch(far2[t1][:], h2[t1], n10_t[:])
                finish(t1)

        for cols, entries in zip(halves, list_halves):
            fetch(far2[last][:, cols], h2[last], n10_t[:, entries])
            nc.vector.tensor_tensor(out=res[last][:, cols], in0=ub2[last][:, cols], in1=far2[last][:, cols], op=ALU.subtract)
        nc.sync.dma_start(out=out_rows[:, last, :], in_=res[last][:])
        for cols in halves:
            nc.vector.tensor_copy(out=res_bf[:, cols, last], in_=res[last][:, cols])
        res_words = tile("res_words", [P, S], U32)
        res_scales = tile("res_scales", [P, S], U8)
        for cols in halves:
            nc.vector.quantize_mx(out=res_words[:, cols].bitcast(FP8X4), scales=res_scales[:, cols], in_=res_bf[:, cols, :].rearrange("p j t -> p (j t)"))
        nc.sync.dma_start(out=out_1[0].rearrange("p c r -> p (c r)").bitcast(I32), in_=res_words[:].bitcast(I32))
        for q in range(4):
            queue = nc.scalar if q % 2 == 0 else nc.sync
            queue.dma_start(out=out_2[0, 4 * q:4 * q + 4, :].bitcast(I32), in_=res_scales[32 * q:32 * q + 4, :].bitcast(I32))
